import numpy as np
import ml_dtypes


def mxq(x, axis, fmt="e4m3"):
    dtype, down = {"e4m3": (ml_dtypes.float8_e4m3fn, 7), "e5m2": (ml_dtypes.float8_e5m2, 14)}[fmt]
    v = np.moveaxis(np.asarray(x, np.float32).astype(ml_dtypes.bfloat16).astype(np.float64), axis, -1)
    blocks = v.reshape(v.shape[:-1] + (-1, 32))
    amax = np.abs(blocks).max(-1, keepdims=True)
    byte = np.maximum(np.where(amax > 0, np.frexp(amax)[1] - 1 + 127, 0) - down, 1)
    scale = np.exp2(byte - 127.0)
    codes = (blocks / scale).astype(np.float32).astype(dtype).astype(np.float64)
    return np.moveaxis((codes * scale).reshape(v.shape), -1, axis)


WIDE = False


def mx_kscale(k):
    if not WIDE:
        return np.ones(k)
    levels = np.array([10, -10, 5, -5, 0])
    if k % 512:
        return np.exp2(np.random.permutation(np.resize(levels, k // 32))).repeat(32)
    a = np.empty((k // 512, 16))
    for p in range(k // 512):
        a[p, :8] = np.random.permutation(np.resize(levels, 8))
        for g in range(8):
            far = levels[np.abs(levels - a[p, g]) >= 10]
            a[p, g + 8] = far[np.random.randint(len(far))]
    return np.exp2(a.ravel()).repeat(32)


BF16 = ml_dtypes.bfloat16


def bf(x):
    return np.asarray(x, np.float32).astype(BF16)


def f64(x):
    return np.asarray(x).astype(np.float64)


E2M1 = np.array([0.0, 0.5, 1.0, 1.5, 2.0, 3.0, 4.0, 6.0, -0.0, -0.5, -1.0, -1.5, -2.0, -3.0, -4.0, -6.0])


def pack_weight(w, fmt):
    k, n = w.shape
    w = f64(bf(w)).reshape(k // 32, 32, n)
    amax = np.abs(w).max(1)
    if fmt == "e4m3":
        byte = np.frexp(amax)[1] - 1 + 127 - 7
    else:
        mant, ex = np.frexp(amax / 6.0)
        byte = np.where(mant > 0.5, ex, ex - 1) + 127
    byte = np.clip(np.where(amax > 0, byte, 1), 1, 254)
    scaled = (w * np.exp2(127.0 - byte)[:, None, :]).reshape(k, n).astype(np.float32)
    by_word = np.ascontiguousarray(scaled.reshape(k // 512, 128, 4, n).transpose(0, 1, 3, 2))
    if fmt == "e4m3":
        words = by_word.astype(ml_dtypes.float8_e4m3fn).view(np.uint8)
    else:
        c = by_word.astype(ml_dtypes.float4_e2m1fn).view(np.uint8) & 0xF
        words = c[..., 0::2] | (c[..., 1::2] << 4)
    return np.ascontiguousarray(words), np.ascontiguousarray(byte.astype(np.uint8).reshape(k // 512, 16, n))


def unpack_weight(words, scales, fmt):
    g, p, n, _ = words.shape
    if fmt == "e4m3":
        vals = np.ascontiguousarray(words).view(ml_dtypes.float8_e4m3fn).astype(np.float64)
    else:
        nib = np.empty((g, p, n, 4), np.uint8)
        nib[..., 0::2] = words & 0xF
        nib[..., 1::2] = words >> 4
        vals = E2M1[nib]
    vals = vals * np.repeat(np.exp2(scales.astype(np.float64) - 127.0), 8, axis=1)[..., None]
    return vals.transpose(0, 1, 3, 2).reshape(g * 512, n)
def pack4(w):
    words, scales = pack_weight(w, "e2m1")
    return words.reshape(words.shape[0], 128, -1), scales


def unpack4(words, scales):
    return unpack_weight(words.reshape(words.shape[0], 128, -1, 2), scales, "e2m1")


def planes(Y):
    n, m = Y.shape
    b = f64(bf(Y)).reshape(n // 32, 32, m)
    amax = np.abs(b).max(1)
    byte = np.clip(np.where(amax > 0, np.frexp(amax)[1] - 1 + 127 - 7, 1), 1, 254)
    codes = (b * np.exp2(127.0 - byte)[:, None, :]).reshape(n, m).astype(np.float32).astype(ml_dtypes.float8_e4m3fn).view(np.uint8)
    words = codes.reshape(n // 512, 128, 4, m).transpose(0, 1, 3, 2)
    return np.ascontiguousarray(words), np.ascontiguousarray(byte.astype(np.uint8).reshape(n // 512, 16, m))


B, D, L, F, C = 4, 256, 1024, 1024, 2


def fourier_matrix(tau):
    theta = np.pi * (np.arange(F) + 0.5) / F
    phase = tau[:, None] * theta[None, :]
    return np.concatenate([np.cos(phase), -np.sin(phase)], axis=1) * np.sqrt(2.0 / L)


def setup_inputs():
    s = mx_kscale(L)
    x = np.random.randn(B, D, L)
    tau = np.arange(L) + 0.2 * np.random.randn(L)
    fourier_words, fourier_scales = pack4(fourier_matrix(tau) / s[:, None])
    magnitude = np.exp(0.8 * np.random.randn(F)) * (1.0 + 0.1 * np.random.randn(D, F))
    angle = np.random.uniform(-np.pi, np.pi, (D, F))
    return {
        "x": bf(x * s),
        "fourier_words": fourier_words,
        "fourier_scales": fourier_scales,
        "response_re": bf(magnitude * np.cos(angle)),
        "response_im": bf(magnitude * np.sin(angle)),
    }


def reference(x, fourier_words, fourier_scales, response_re, response_im):
    xq = mxq(f64(x).reshape(B * D, L), 1, "e4m3")
    W = unpack4(fourier_words, fourier_scales)
    P = (xq @ W).reshape(B, D, C, F)
    hr = f64(response_re)[:, None, :]
    hi = f64(response_im)
    cross = np.stack([-hi, hi], axis=1)
    y = P * hr + P[:, :, ::-1] * cross
    Y = y.reshape(B * D * C, F).T
    words, scales = planes(Y)
    return y, words, scales

@@ -1,0 +1,253 @@
+from contextlib import ExitStack
+
+import concourse.mybir as mybir
+from concourse.masks import make_identity
+
+B, D, L, F, C = 4, 256, 1024, 1024, 2
+FLOPS = 2 * B * D * L * C * F
+
+F32 = mybir.dt.float32
+BF16 = mybir.dt.bfloat16
+I32 = mybir.dt.int32
+U32 = mybir.dt.uint32
+U8 = mybir.dt.uint8
+FP8X4 = mybir.dt.float8_e4m3fn_x4
+FP4X4 = mybir.dt.float4_e2m1fn_x4
+MULT = mybir.AluOpType.mult
+ADD = mybir.AluOpType.add
+
+P = 128
+KG = 512
+ROW_TILES = B * D // P
+D_TILES = D // P
+K_GROUPS = L // KG
+F_GROUPS = F // KG
+UNITS = ROW_TILES * F_GROUPS
+M_UNIT = P * C
+
+
+def tile_jittered_fourier_frequency_response_g4_kernel(
+    tc, x, fourier_words, fourier_scales, response_re, response_im, out_0, out_1, out_2
+):
+    nc = tc.nc
+    x_rows = x.rearrange("b d j -> (b d) j")
+    y_rows = out_0.rearrange("b d c f -> (b d) c f")
+
+    with ExitStack() as ctx:
+        keep = ctx.enter_context(tc.tile_pool(name="keep", bufs=1))
+        work = ctx.enter_context(tc.tile_pool(name="work", bufs=3))
+        psum = ctx.enter_context(tc.psum_pool(name="psum", bufs=2))
+        ctx.enter_context(tc.manual_schedule())
+
+        ident = keep.tile([P, P], F32, name="ident")
+        w_scales = keep.tile([P, K_GROUPS, C * F], U8, name="w_scales", align_bytes=64)
+        x_raw = [keep.tile([P, L], BF16, name="x_raw%d" % r, align_bytes=64) for r in range(ROW_TILES)]
+        w_words = {}
+        resp = {}
+        for fg in range(F_GROUPS):
+            for c in range(C):
+                w_words[c, fg] = keep.tile([P, K_GROUPS, 2 * KG], U8, name="w_words%d%d" % (c, fg), align_bytes=64)
+            for dt in range(D_TILES):
+                resp[dt, fg] = keep.tile([P, C, KG], BF16, name="resp%d%d" % (dt, fg), align_bytes=64)
+        x_grouped = keep.tile([P, ROW_TILES, L], BF16, name="x_grouped", align_bytes=64)
+        x_codes = keep.tile([P, ROW_TILES, K_GROUPS * P], U32, name="x_codes", align_bytes=64)
+        x_scales = keep.tile([P, ROW_TILES, K_GROUPS * P], U8, name="x_scales", align_bytes=64)
+        y_grouped = keep.tile([P, UNITS, 4 * M_UNIT], BF16, name="y_grouped", align_bytes=64)
+        y_codes = keep.tile([P, UNITS, M_UNIT], U32, name="y_codes", align_bytes=64)
+        y_scales = keep.tile([P, UNITS, M_UNIT], U8, name="y_scales", align_bytes=64)
+
+        nc.vector.memset(w_scales[:].rearrange("p g n -> p (g n)").bitcast(I32), 0)
+        make_identity(nc, ident[:])
+
+        def load_x(r):
+            nc.sync.dma_start(out=x_raw[r][:], in_=x_rows[r * P:(r + 1) * P, :])
+
+        def load_w(c, fg):
+            b0 = 2 * (c * F + fg * KG)
+            nc.sync.dma_start(
+                out=w_words[c, fg][:].bitcast(I32),
+                in_=fourier_words[:, :, b0:b0 + 2 * KG].rearrange("g p n -> p g n").bitcast(I32),
+            )
+
+        def load_resp(dt, fg):
+            for i, src in enumerate((response_re, response_im)):
+                nc.sync.dma_start(
+                    out=resp[dt, fg][:, i, :], in_=src[dt * P:(dt + 1) * P, fg * KG:(fg + 1) * KG]
+                )
+
+        load_x(0)
+        for q in range(4):
+            nc.sync.dma_start(
+                out=w_scales[32 * q:32 * q + 4, :, :].bitcast(I32),
+                in_=fourier_scales[:, 4 * q:4 * q + 4, :].rearrange("g r n -> r g n").bitcast(I32),
+            )
+        load_x(1)
+        load_w(0, 0)
+        load_w(1, 0)
+        load_resp(0, 0)
+        load_x(2)
+        load_resp(1, 0)
+        for r in range(3, ROW_TILES):
+            load_x(r)
+        load_w(0, 1)
+        load_w(1, 1)
+        load_resp(0, 1)
+        load_resp(1, 1)
+
+        x_turned = {}
+        sums = {}
+        terms = {}
+        y = {}
+        y_bf = {}
+        y_turned = {}
+
+        def transpose_x(r):
+            bank = psum.tile([P, K_GROUPS, 2, P], F32, name="turned", tag="turned", bufs=4)
+            words = x_raw[r][:].bitcast(F32)
+            for g in range(K_GROUPS):
+                for u in range(2):
+                    nc.tensor.transpose(bank[:, g, u, :], words[:, 256 * g + u:256 * (g + 1):2], ident[:])
+            x_turned[r] = bank
+
+        def copy_x(r):
+            nc.scalar.copy(
+                out=x_grouped[:, r, :].bitcast(F32).rearrange("p (g r u) -> p g r u", g=K_GROUPS, u=2),
+                in_=x_turned[r][:].rearrange("p g u r -> p g r u"),
+            )
+
+        def quantise_x(r0, r1):
+            nc.vector.quantize_mx(
+                out=x_codes[:, r0:r1, :].rearrange("p r n -> p (r n)").bitcast(FP8X4),
+                scales=x_scales[:, r0:r1, :].rearrange("p r n -> p (r n)"),
+                in_=x_grouped[:, r0:r1, :].rearrange("p r n -> p (r n)"),
+            )
+
+        def multiply(s):
+            fg, r = divmod(s, ROW_TILES)
+            for c in range(C):
+                acc = psum.tile([P, KG], F32, name="acc%d" % c, tag="acc%d" % c, bufs=2)
+                n0 = c * F + fg * KG
+                for g in range(K_GROUPS):
+                    nc.tensor.matmul_mx(
+                        out=acc[:],
+                        lhsT=x_codes[:, r, g * P:(g + 1) * P].bitcast(FP8X4),
+                        lhsT_scale=x_scales[:, r, g * P:(g + 1) * P],
+                        rhs=w_words[c, fg][:, g, :].bitcast(FP4X4),
+                        rhs_scale=w_scales[:, g, n0:n0 + KG],
+                        start=(g == 0),
+                        stop=(g == K_GROUPS - 1),
+                    )
+                sums[s, c] = acc
+
+        def products(s):
+            fg, r = divmod(s, ROW_TILES)
+            h = resp[r % D_TILES, fg]
+            t = work.tile([P, 2, C, KG], F32, name="terms", tag="terms", bufs=3)
+            nc.vector.tensor_tensor(out=t[:, 0, 0, :], in0=sums[s, 0][:], in1=h[:, 0, :], op=MULT)
+            nc.vector.tensor_tensor(out=t[:, 0, 1, :], in0=sums[s, 0][:], in1=h[:, 1, :], op=MULT)
+            nc.vector.scalar_tensor_tensor(
+                out=t[:, 1, 0, :], in0=sums[s, 1][:], scalar=-1.0, in1=h[:, 1, :], op0=MULT, op1=MULT
+            )
+            nc.vector.tensor_tensor(out=t[:, 1, 1, :], in0=sums[s, 1][:], in1=h[:, 0, :], op=MULT)
+            terms[s] = t
+
+        def store_y(s):
+            fg, r = divmod(s, ROW_TILES)
+            nc.sync.dma_start(out=y_rows[r * P:(r + 1) * P, :, fg * KG:(fg + 1) * KG], in_=y[s][:])
+
+        def add_terms(s):
+            y[s] = work.tile([P, C, KG], F32, name="y", tag="y", bufs=4)
+            nc.gpsimd.tensor_tensor(out=y[s][:], in0=terms[s][:, 0, :, :], in1=terms[s][:, 1, :, :], op=ADD)
+            store_y(s)
+
+        def round_y(s, copy):
+            y_bf[s] = work.tile([P, C, KG], BF16, name="y_bf", tag="y_bf", bufs=3, align_bytes=64)
+            for c in range(C):
+                copy(
+                    out=y_bf[s][:, c, :].rearrange("r (u p e) -> r u p e", u=2, e=2),
+                    in_=y[s][:, c, :].rearrange("r (p u e) -> r u p e", u=2, e=2),
+                )
+
+        def transpose_y(s):
+            bank = psum.tile([P, C, 2, P], F32, name="turned", tag="turned", bufs=4)
+            for c in range(C):
+                words = y_bf[s][:, c, :].bitcast(F32)
+                for u in range(2):
+                    nc.tensor.transpose(bank[:, c, u, :], words[:, u * P:(u + 1) * P], ident[:])
+            y_turned[s] = bank
+
+        def copy_y(s):
+            nc.scalar.copy(
+                out=y_grouped[:, s, :].bitcast(F32).rearrange("p (r w) -> p r w", w=2 * C),
+                in_=y_turned[s][:].rearrange("p c u r -> p r (c u)"),
+            )
+
+        def quantise_y(s0, s1):
+            nc.vector.quantize_mx(
+                out=y_codes[:, s0:s1, :].rearrange("p s m -> p (s m)").bitcast(FP8X4),
+                scales=y_scales[:, s0:s1, :].rearrange("p s m -> p (s m)"),
+                in_=y_grouped[:, s0:s1, :].rearrange("p s m -> p (s m)"),
+            )
+            fg, r0 = divmod(s0, ROW_TILES)
+            m0, m1 = r0 * M_UNIT, (r0 + s1 - s0) * M_UNIT
+            nc.sync.dma_start(
+                out=out_1[fg].rearrange("p m t -> p (m t)")[:, 4 * m0:4 * m1].bitcast(I32),
+                in_=y_codes[:, s0:s1, :].rearrange("p s m -> p (s m)").bitcast(I32),
+            )
+            if s1 % ROW_TILES == 0:
+                for q in range(4):
+                    queue = nc.scalar if (s1 == UNITS and q % 2) else nc.sync
+                    rows = y_scales[32 * q:32 * q + 4, fg * ROW_TILES:s1, :]
+                    queue.dma_start(
+                        out=out_2[fg, 4 * q:4 * q + 4, :].bitcast(I32),
+                        in_=rows.rearrange("p s m -> p (s m)").bitcast(I32),
+                    )
+
+        x_turns = {0: [3], 1: [4, 5], 2: [6], 3: [7]}
+        x_quants = {0: (2, 3), 1: (3, 4), 2: (4, 6), 4: (6, 8)}
+        y_quants = {3: (0, 1), 5: (1, 3)}
+        for s in range(6, UNITS - 1):
+            y_quants[s] = (s - 3, s - 2)
+
+        transpose_x(0)
+        copy_x(0)
+        transpose_x(1)
+        copy_x(1)
+        quantise_x(0, 1)
+        multiply(0)
+        quantise_x(1, 2)
+        transpose_x(2)
+        copy_x(2)
+
+        for s in range(UNITS):
+            if s >= 2:
+                round_y(s - 2, nc.scalar.copy)
+            if s + 1 < UNITS:
+                multiply(s + 1)
+            if s >= 1:
+                add_terms(s - 1)
+            products(s)
+            for r in x_turns.get(s, []):
+                transpose_x(r)
+                copy_x(r)
+            if s >= 2:
+                transpose_y(s - 2)
+                copy_y(s - 2)
+            if s in x_quants:
+                quantise_x(*x_quants[s])
+            if s in y_quants:
+                quantise_y(*y_quants[s])
+
+        last = UNITS - 1
+        round_y(last - 1, nc.scalar.copy)
+        y[last] = work.tile([P, C, KG], F32, name="y", tag="y", bufs=4)
+        nc.vector.tensor_tensor(out=y[last][:], in0=terms[last][:, 0, :, :], in1=terms[last][:, 1, :, :], op=ADD)
+        store_y(last)
+        round_y(last, nc.vector.tensor_copy)
+        transpose_y(last - 1)
+        copy_y(last - 1)
+        transpose_y(last)
+        copy_y(last)
+        quantise_y(last - 3, last - 1)
+        quantise_y(last - 1, last)
+        quantise_y(last, UNITS)

@@ -49,15 +49,14 @@ def tile_jittered_fourier_frequency_response_g4_kernel(
                 w_words[c, fg] = keep.tile([P, K_GROUPS, 2 * KG], U8, name="w_words%d%d" % (c, fg), align_bytes=64)
             for dt in range(D_TILES):
                 resp[dt, fg] = keep.tile([P, C, KG], BF16, name="resp%d%d" % (dt, fg), align_bytes=64)
-        x_grouped = keep.tile([P, ROW_TILES, L], BF16, name="x_grouped", align_bytes=64)
-        x_codes = keep.tile([P, ROW_TILES, K_GROUPS * P], U32, name="x_codes", align_bytes=64)
-        x_scales = keep.tile([P, ROW_TILES, K_GROUPS * P], U8, name="x_scales", align_bytes=64)
-        y_grouped = keep.tile([P, UNITS, 4 * M_UNIT], BF16, name="y_grouped", align_bytes=64)
-        y_codes = keep.tile([P, UNITS, M_UNIT], U32, name="y_codes", align_bytes=64)
-        y_scales = keep.tile([P, UNITS, M_UNIT], U8, name="y_scales", align_bytes=64)
+        x_grouped = keep.tile([P, ROW_TILES * L], BF16, name="x_grouped", align_bytes=64)
+        x_codes = keep.tile([P, ROW_TILES * K_GROUPS * P], U32, name="x_codes", align_bytes=64)
+        x_scales = keep.tile([P, ROW_TILES * K_GROUPS * P], U8, name="x_scales", align_bytes=64)
+        y_grouped = keep.tile([P, F_GROUPS, ROW_TILES * M_UNIT * 4], BF16, name="y_grouped", align_bytes=64)
+        y_codes = keep.tile([P, F_GROUPS, ROW_TILES * M_UNIT], U32, name="y_codes", align_bytes=64)
+        y_scales = keep.tile([P, F_GROUPS, ROW_TILES * M_UNIT], U8, name="y_scales", align_bytes=64)
 
         nc.vector.memset(w_scales[:].rearrange("p g n -> p (g n)").bitcast(I32), 0)
-        make_identity(nc, ident[:])
 
         def load_x(r):
             nc.sync.dma_start(out=x_raw[r][:], in_=x_rows[r * P:(r + 1) * P, :])
@@ -69,90 +68,98 @@ def tile_jittered_fourier_frequency_response_g4_kernel(
                 in_=fourier_words[:, :, b0:b0 + 2 * KG].rearrange("g p n -> p g n").bitcast(I32),
             )
 
-        def load_resp(dt, fg):
+        def load_resp(dt, fg, queue=nc.sync):
             for i, src in enumerate((response_re, response_im)):
-                nc.sync.dma_start(
+                queue.dma_start(
                     out=resp[dt, fg][:, i, :], in_=src[dt * P:(dt + 1) * P, fg * KG:(fg + 1) * KG]
                 )
 
+        def load_scales(plane, n0, n1, queue):
+            for q in range(4):
+                queue.dma_start(
+                    out=plane[32 * q:32 * q + 4, :, :].bitcast(I32),
+                    in_=fourier_scales[:, 4 * q:4 * q + 4, n0:n1].rearrange("g r n -> r g n").bitcast(I32),
+                )
+
+        make_identity(nc, ident[:])
         load_x(0)
-        for q in range(4):
-            nc.sync.dma_start(
-                out=w_scales[32 * q:32 * q + 4, :, :].bitcast(I32),
-                in_=fourier_scales[:, 4 * q:4 * q + 4, :].rearrange("g r n -> r g n").bitcast(I32),
-            )
         load_x(1)
         load_w(0, 0)
+        load_scales(w_scales, 0, C * F, nc.sync)
         load_w(1, 0)
         load_resp(0, 0)
+        load_w(0, 1)
+        load_resp(0, 1)
+        load_w(1, 1)
         load_x(2)
         load_resp(1, 0)
+        load_resp(1, 1)
         for r in range(3, ROW_TILES):
             load_x(r)
-        load_w(0, 1)
-        load_w(1, 1)
-        load_resp(0, 1)
-        load_resp(1, 1)
 
-        x_turned = {}
+        turned = {}
         sums = {}
         terms = {}
         y = {}
         y_bf = {}
-        y_turned = {}
 
-        def transpose_x(r):
+        def turn_x(r, g0, g1):
             bank = psum.tile([P, K_GROUPS, 2, P], F32, name="turned", tag="turned", bufs=4)
             words = x_raw[r][:].bitcast(F32)
-            for g in range(K_GROUPS):
+            for g in range(g0, g1):
                 for u in range(2):
                     nc.tensor.transpose(bank[:, g, u, :], words[:, 256 * g + u:256 * (g + 1):2], ident[:])
-            x_turned[r] = bank
+            turned["x", r, g0] = bank
 
-        def copy_x(r):
+        def copy_x(r, g0, g1):
+            bank = turned["x", r, g0]
+            grouped = x_grouped[:, r * L + g0 * KG:r * L + g1 * KG]
             nc.scalar.copy(
-                out=x_grouped[:, r, :].bitcast(F32).rearrange("p (g r u) -> p g r u", g=K_GROUPS, u=2),
-                in_=x_turned[r][:].rearrange("p g u r -> p g r u"),
+                out=grouped.bitcast(F32).rearrange("p (g r u) -> p g r u", g=g1 - g0, u=2),
+                in_=bank[:, g0:g1, :, :].rearrange("p g u r -> p g r u"),
             )
 
-        def quantise_x(r0, r1):
+        def quantise_x(j0, j1):
             nc.vector.quantize_mx(
-                out=x_codes[:, r0:r1, :].rearrange("p r n -> p (r n)").bitcast(FP8X4),
-                scales=x_scales[:, r0:r1, :].rearrange("p r n -> p (r n)"),
-                in_=x_grouped[:, r0:r1, :].rearrange("p r n -> p (r n)"),
+                out=x_codes[:, j0 * P:j1 * P].bitcast(FP8X4),
+                scales=x_scales[:, j0 * P:j1 * P],
+                in_=x_grouped[:, j0 * KG:j1 * KG],
             )
 
-        def multiply(s):
-            fg, r = divmod(s, ROW_TILES)
-            for c in range(C):
-                acc = psum.tile([P, KG], F32, name="acc%d" % c, tag="acc%d" % c, bufs=2)
-                n0 = c * F + fg * KG
-                for g in range(K_GROUPS):
-                    nc.tensor.matmul_mx(
-                        out=acc[:],
-                        lhsT=x_codes[:, r, g * P:(g + 1) * P].bitcast(FP8X4),
-                        lhsT_scale=x_scales[:, r, g * P:(g + 1) * P],
-                        rhs=w_words[c, fg][:, g, :].bitcast(FP4X4),
-                        rhs_scale=w_scales[:, g, n0:n0 + KG],
-                        start=(g == 0),
-                        stop=(g == K_GROUPS - 1),
-                    )
-                sums[s, c] = acc
+        def multiply(s, c):
+            r, fg = divmod(s, F_GROUPS)
+            acc = psum.tile([P, KG], F32, name="acc%d" % c, tag="acc%d" % c, bufs=2)
+            n0 = c * F + fg * KG
+            for g in range(K_GROUPS):
+                j = r * K_GROUPS + g
+                nc.tensor.matmul_mx(
+                    out=acc[:],
+                    lhsT=x_codes[:, j * P:(j + 1) * P].bitcast(FP8X4),
+                    lhsT_scale=x_scales[:, j * P:(j + 1) * P],
+                    rhs=w_words[c, fg][:, g, :].bitcast(FP4X4),
+                    rhs_scale=w_scales[:, g, n0:n0 + KG],
+                    start=(g == 0),
+                    stop=(g == K_GROUPS - 1),
+                )
+            sums[s, c] = acc
 
-        def products(s):
-            fg, r = divmod(s, ROW_TILES)
+        def product(s, c_in, c_out):
+            r, fg = divmod(s, F_GROUPS)
             h = resp[r % D_TILES, fg]
-            t = work.tile([P, 2, C, KG], F32, name="terms", tag="terms", bufs=3)
-            nc.vector.tensor_tensor(out=t[:, 0, 0, :], in0=sums[s, 0][:], in1=h[:, 0, :], op=MULT)
-            nc.vector.tensor_tensor(out=t[:, 0, 1, :], in0=sums[s, 0][:], in1=h[:, 1, :], op=MULT)
-            nc.vector.scalar_tensor_tensor(
-                out=t[:, 1, 0, :], in0=sums[s, 1][:], scalar=-1.0, in1=h[:, 1, :], op0=MULT, op1=MULT
-            )
-            nc.vector.tensor_tensor(out=t[:, 1, 1, :], in0=sums[s, 1][:], in1=h[:, 0, :], op=MULT)
-            terms[s] = t
+            if s not in terms:
+                terms[s] = work.tile([P, C, C, KG], F32, name="terms", tag="terms", bufs=3)
+            out = terms[s][:, c_in, c_out, :]
+            if c_in == c_out:
+                nc.vector.tensor_tensor(out=out, in0=sums[s, c_in][:], in1=h[:, 0, :], op=MULT)
+            elif c_in == 0:
+                nc.vector.tensor_tensor(out=out, in0=sums[s, c_in][:], in1=h[:, 1, :], op=MULT)
+            else:
+                nc.vector.scalar_tensor_tensor(
+                    out=out, in0=sums[s, c_in][:], scalar=-1.0, in1=h[:, 1, :], op0=MULT, op1=MULT
+                )
 
         def store_y(s):
-            fg, r = divmod(s, ROW_TILES)
+            r, fg = divmod(s, F_GROUPS)
             nc.sync.dma_start(out=y_rows[r * P:(r + 1) * P, :, fg * KG:(fg + 1) * KG], in_=y[s][:])
 
         def add_terms(s):
@@ -160,94 +167,128 @@ def tile_jittered_fourier_frequency_response_g4_kernel(
             nc.gpsimd.tensor_tensor(out=y[s][:], in0=terms[s][:, 0, :, :], in1=terms[s][:, 1, :, :], op=ADD)
             store_y(s)
 
-        def round_y(s, copy):
+        def round_y(s):
             y_bf[s] = work.tile([P, C, KG], BF16, name="y_bf", tag="y_bf", bufs=3, align_bytes=64)
             for c in range(C):
-                copy(
+                nc.scalar.copy(
                     out=y_bf[s][:, c, :].rearrange("r (u p e) -> r u p e", u=2, e=2),
                     in_=y[s][:, c, :].rearrange("r (p u e) -> r u p e", u=2, e=2),
                 )
 
-        def transpose_y(s):
+        def turn_y(s):
             bank = psum.tile([P, C, 2, P], F32, name="turned", tag="turned", bufs=4)
             for c in range(C):
                 words = y_bf[s][:, c, :].bitcast(F32)
                 for u in range(2):
                     nc.tensor.transpose(bank[:, c, u, :], words[:, u * P:(u + 1) * P], ident[:])
-            y_turned[s] = bank
+            turned["y", s] = bank
 
         def copy_y(s):
+            r, fg = divmod(s, F_GROUPS)
+            bank = turned["y", s]
+            grouped = y_grouped[:, fg, r * M_UNIT * 4:(r + 1) * M_UNIT * 4]
             nc.scalar.copy(
-                out=y_grouped[:, s, :].bitcast(F32).rearrange("p (r w) -> p r w", w=2 * C),
-                in_=y_turned[s][:].rearrange("p c u r -> p r (c u)"),
+                out=grouped.bitcast(F32).rearrange("p (r w) -> p r w", w=2 * C),
+                in_=bank[:].rearrange("p c u r -> p r (c u)"),
             )
 
-        def quantise_y(s0, s1):
+        def quantise_y(fg, r0, r1):
+            m0, m1 = r0 * M_UNIT, r1 * M_UNIT
             nc.vector.quantize_mx(
-                out=y_codes[:, s0:s1, :].rearrange("p s m -> p (s m)").bitcast(FP8X4),
-                scales=y_scales[:, s0:s1, :].rearrange("p s m -> p (s m)"),
-                in_=y_grouped[:, s0:s1, :].rearrange("p s m -> p (s m)"),
+                out=y_codes[:, fg, m0:m1].bitcast(FP8X4),
+                scales=y_scales[:, fg, m0:m1],
+                in_=y_grouped[:, fg, 4 * m0:4 * m1],
             )
-            fg, r0 = divmod(s0, ROW_TILES)
-            m0, m1 = r0 * M_UNIT, (r0 + s1 - s0) * M_UNIT
+
+        def store_codes(fg, r0, r1):
+            m0, m1 = r0 * M_UNIT, r1 * M_UNIT
             nc.sync.dma_start(
                 out=out_1[fg].rearrange("p m t -> p (m t)")[:, 4 * m0:4 * m1].bitcast(I32),
-                in_=y_codes[:, s0:s1, :].rearrange("p s m -> p (s m)").bitcast(I32),
+                in_=y_codes[:, fg, m0:m1].bitcast(I32),
             )
-            if s1 % ROW_TILES == 0:
-                for q in range(4):
-                    queue = nc.scalar if (s1 == UNITS and q % 2) else nc.sync
-                    rows = y_scales[32 * q:32 * q + 4, fg * ROW_TILES:s1, :]
-                    queue.dma_start(
-                        out=out_2[fg, 4 * q:4 * q + 4, :].bitcast(I32),
-                        in_=rows.rearrange("p s m -> p (s m)").bitcast(I32),
-                    )
 
-        x_turns = {0: [3], 1: [4, 5], 2: [6], 3: [7]}
-        x_quants = {0: (2, 3), 1: (3, 4), 2: (4, 6), 4: (6, 8)}
-        y_quants = {3: (0, 1), 5: (1, 3)}
-        for s in range(6, UNITS - 1):
-            y_quants[s] = (s - 3, s - 2)
+        def store_scales(r0, r1, queues):
+            m0, m1 = r0 * M_UNIT, r1 * M_UNIT
+            for q in range(4):
+                queues[q % len(queues)].dma_start(
+                    out=out_2[:, 4 * q:4 * q + 4, m0:m1].rearrange("g r m -> r g m").bitcast(I32),
+                    in_=y_scales[32 * q:32 * q + 4, :, m0:m1].bitcast(I32),
+                )
 
-        transpose_x(0)
-        copy_x(0)
-        transpose_x(1)
-        copy_x(1)
-        quantise_x(0, 1)
-        multiply(0)
-        quantise_x(1, 2)
-        transpose_x(2)
-        copy_x(2)
+        x_turns = {1: [2], 2: [3, 4], 4: [5], 5: [6], 8: [7]}
+        x_quants = {2: (2, 3), 4: (3, 5), 8: (5, 7), 12: (7, 8)}
+        y_quants = {}
+        for r0 in range(0, ROW_TILES - 2, 2):
+            y_quants[2 * r0 + 3] = (0, r0, r0 + 1)
+            y_quants[2 * r0 + 5] = (0, r0 + 1, r0 + 2)
+            y_quants[2 * r0 + 6] = (1, r0, r0 + 2)
+
+        for g in range(K_GROUPS):
+            turn_x(0, g, g + 1)
+            copy_x(0, g, g + 1)
+        for g in range(K_GROUPS):
+            quantise_x(g, g + 1)
+        turn_x(1, 0, K_GROUPS)
+        copy_x(1, 0, K_GROUPS)
+        quantise_x(K_GROUPS, 2 * K_GROUPS)
+        multiply(0, 0)
+        multiply(0, 1)
 
         for s in range(UNITS):
             if s >= 2:
-                round_y(s - 2, nc.scalar.copy)
+                round_y(s - 2)
+            if s >= 3:
+                copy_y(s - 3)
+            for r in x_turns.get(s - 1, []):
+                copy_x(r, 0, K_GROUPS)
             if s + 1 < UNITS:
-                multiply(s + 1)
+                multiply(s + 1, 0)
+                multiply(s + 1, 1)
+            for r in x_turns.get(s, []):
+                turn_x(r, 0, K_GROUPS)
+            if s >= 2:
+                turn_y(s - 2)
             if s >= 1:
                 add_terms(s - 1)
-            products(s)
-            for r in x_turns.get(s, []):
-                transpose_x(r)
-                copy_x(r)
-            if s >= 2:
-                transpose_y(s - 2)
-                copy_y(s - 2)
+            for c_in in range(C):
+                for c_out in range(C):
+                    product(s, c_in, c_out)
             if s in x_quants:
-                quantise_x(*x_quants[s])
+                r0, r1 = x_quants[s]
+                quantise_x(r0 * K_GROUPS, r1 * K_GROUPS)
             if s in y_quants:
                 quantise_y(*y_quants[s])
+                store_codes(*y_quants[s])
+            if s == UNITS - 2:
+                store_scales(0, ROW_TILES - 2, [nc.sync])
 
         last = UNITS - 1
-        round_y(last - 1, nc.scalar.copy)
+        r_last = ROW_TILES - 1
+        copy_y(last - 2)
+        round_y(last - 1)
+        y_bf[last] = work.tile([P, C, KG], BF16, name="y_bf", tag="y_bf", bufs=3, align_bytes=64)
+        for c in range(C):
+            nc.vector.tensor_tensor(
+                out=y_bf[last][:, c, :].rearrange("r (u p e) -> r u p e", u=2, e=2),
+                in0=terms[last][:, 0, c, :].rearrange("r (p u e) -> r u p e", u=2, e=2),
+                in1=terms[last][:, 1, c, :].rearrange("r (p u e) -> r u p e", u=2, e=2),
+                op=ADD,
+            )
         y[last] = work.tile([P, C, KG], F32, name="y", tag="y", bufs=4)
         nc.vector.tensor_tensor(out=y[last][:], in0=terms[last][:, 0, :, :], in1=terms[last][:, 1, :, :], op=ADD)
         store_y(last)
-        round_y(last, nc.vector.tensor_copy)
-        transpose_y(last - 1)
-        copy_y(last - 1)
-        transpose_y(last)
+        turn_y(last)
         copy_y(last)
-        quantise_y(last - 3, last - 1)
-        quantise_y(last - 1, last)
-        quantise_y(last, UNITS)
+        turn_y(last - 1)
+        copy_y(last - 1)
+        for fg in range(F_GROUPS):
+            quantise_y(fg, r_last - 1, r_last)
+        m0, m1 = (r_last - 1) * M_UNIT, r_last * M_UNIT
+        nc.sync.dma_start(
+            out=out_1.rearrange("g p m t -> p g (m t)")[:, :, 4 * m0:4 * m1].bitcast(I32),
+            in_=y_codes[:, :, m0:m1].bitcast(I32),
+        )
+        for fg in (1, 0):
+            quantise_y(fg, r_last, r_last + 1)
+            store_codes(fg, r_last, r_last + 1)
+        store_scales(ROW_TILES - 2, ROW_TILES, [nc.scalar, nc.sync])

from contextlib import ExitStack

import concourse.mybir as mybir
from concourse.masks import make_identity

B, D, L, F, C = 4, 256, 1024, 1024, 2
FLOPS = 2 * B * D * L * C * F

F32 = mybir.dt.float32
BF16 = mybir.dt.bfloat16
I32 = mybir.dt.int32
U32 = mybir.dt.uint32
U8 = mybir.dt.uint8
FP8X4 = mybir.dt.float8_e4m3fn_x4
FP4X4 = mybir.dt.float4_e2m1fn_x4
MULT = mybir.AluOpType.mult
ADD = mybir.AluOpType.add

P = 128
KG = 512
ROW_TILES = B * D // P
D_TILES = D // P
K_GROUPS = L // KG
F_GROUPS = F // KG
UNITS = ROW_TILES * F_GROUPS
M_UNIT = P * C


def tile_jittered_fourier_frequency_response_g4_kernel(
    tc, x, fourier_words, fourier_scales, response_re, response_im, out_0, out_1, out_2
):
    nc = tc.nc
    x_rows = x.rearrange("b d j -> (b d) j")
    y_rows = out_0.rearrange("b d c f -> (b d) c f")

    with ExitStack() as ctx:
        keep = ctx.enter_context(tc.tile_pool(name="keep", bufs=1))
        work = ctx.enter_context(tc.tile_pool(name="work", bufs=3))
        psum = ctx.enter_context(tc.psum_pool(name="psum", bufs=2))
        ctx.enter_context(tc.manual_schedule())

        ident = keep.tile([P, P], F32, name="ident")
        w_scales = keep.tile([P, K_GROUPS, C * F], U8, name="w_scales", align_bytes=64)
        x_raw = [keep.tile([P, L], BF16, name="x_raw%d" % r, align_bytes=64) for r in range(ROW_TILES)]
        w_words = {}
        resp = {}
        for fg in range(F_GROUPS):
            for c in range(C):
                w_words[c, fg] = keep.tile([P, K_GROUPS, 2 * KG], U8, name="w_words%d%d" % (c, fg), align_bytes=64)
            for dt in range(D_TILES):
                resp[dt, fg] = keep.tile([P, C, KG], BF16, name="resp%d%d" % (dt, fg), align_bytes=64)
        x_grouped = keep.tile([P, ROW_TILES * L], BF16, name="x_grouped", align_bytes=64)
        x_codes = keep.tile([P, ROW_TILES * K_GROUPS * P], U32, name="x_codes", align_bytes=64)
        x_scales = keep.tile([P, ROW_TILES * K_GROUPS * P], U8, name="x_scales", align_bytes=64)
        y_grouped = keep.tile([P, F_GROUPS, ROW_TILES * M_UNIT * 4], BF16, name="y_grouped", align_bytes=64)
        y_codes = keep.tile([P, F_GROUPS, ROW_TILES * M_UNIT], U32, name="y_codes", align_bytes=64)
        y_scales = keep.tile([P, F_GROUPS, ROW_TILES * M_UNIT], U8, name="y_scales", align_bytes=64)

        nc.vector.memset(w_scales[:].rearrange("p g n -> p (g n)").bitcast(I32), 0)

        def load_x(r):
            nc.sync.dma_start(out=x_raw[r][:], in_=x_rows[r * P:(r + 1) * P, :])

        def load_w(c, fg):
            b0 = 2 * (c * F + fg * KG)
            nc.sync.dma_start(
                out=w_words[c, fg][:].bitcast(I32),
                in_=fourier_words[:, :, b0:b0 + 2 * KG].rearrange("g p n -> p g n").bitcast(I32),
            )

        def load_resp(dt, fg, queue=nc.sync):
            for i, src in enumerate((response_re, response_im)):
                queue.dma_start(
                    out=resp[dt, fg][:, i, :], in_=src[dt * P:(dt + 1) * P, fg * KG:(fg + 1) * KG]
                )

        def load_scales(plane, n0, n1, queue):
            for q in range(4):
                queue.dma_start(
                    out=plane[32 * q:32 * q + 4, :, :].bitcast(I32),
                    in_=fourier_scales[:, 4 * q:4 * q + 4, n0:n1].rearrange("g r n -> r g n").bitcast(I32),
                )

        make_identity(nc, ident[:])
        load_x(0)
        load_x(1)
        load_w(0, 0)
        load_scales(w_scales, 0, C * F, nc.sync)
        load_w(1, 0)
        load_resp(0, 0)
        load_w(0, 1)
        load_resp(0, 1)
        load_w(1, 1)
        load_x(2)
        load_resp(1, 0)
        load_resp(1, 1)
        for r in range(3, ROW_TILES):
            load_x(r)

        turned = {}
        sums = {}
        terms = {}
        y = {}
        y_bf = {}

        def turn_x(r, g0, g1):
            bank = psum.tile([P, K_GROUPS, 2, P], F32, name="turned", tag="turned", bufs=4)
            words = x_raw[r][:].bitcast(F32)
            for g in range(g0, g1):
                for u in range(2):
                    nc.tensor.transpose(bank[:, g, u, :], words[:, 256 * g + u:256 * (g + 1):2], ident[:])
            turned["x", r, g0] = bank

        def copy_x(r, g0, g1):
            bank = turned["x", r, g0]
            grouped = x_grouped[:, r * L + g0 * KG:r * L + g1 * KG]
            nc.scalar.copy(
                out=grouped.bitcast(F32).rearrange("p (g r u) -> p g r u", g=g1 - g0, u=2),
                in_=bank[:, g0:g1, :, :].rearrange("p g u r -> p g r u"),
            )

        def quantise_x(j0, j1):
            nc.vector.quantize_mx(
                out=x_codes[:, j0 * P:j1 * P].bitcast(FP8X4),
                scales=x_scales[:, j0 * P:j1 * P],
                in_=x_grouped[:, j0 * KG:j1 * KG],
            )

        def multiply(s, c):
            r, fg = divmod(s, F_GROUPS)
            acc = psum.tile([P, KG], F32, name="acc%d" % c, tag="acc%d" % c, bufs=2)
            n0 = c * F + fg * KG
            for g in range(K_GROUPS):
                j = r * K_GROUPS + g
                nc.tensor.matmul_mx(
                    out=acc[:],
                    lhsT=x_codes[:, j * P:(j + 1) * P].bitcast(FP8X4),
                    lhsT_scale=x_scales[:, j * P:(j + 1) * P],
                    rhs=w_words[c, fg][:, g, :].bitcast(FP4X4),
                    rhs_scale=w_scales[:, g, n0:n0 + KG],
                    start=(g == 0),
                    stop=(g == K_GROUPS - 1),
                )
            sums[s, c] = acc

        def product(s, c_in, c_out):
            r, fg = divmod(s, F_GROUPS)
            h = resp[r % D_TILES, fg]
            if s not in terms:
                terms[s] = work.tile([P, C, C, KG], F32, name="terms", tag="terms", bufs=3)
            out = terms[s][:, c_in, c_out, :]
            if c_in == c_out:
                nc.vector.tensor_tensor(out=out, in0=sums[s, c_in][:], in1=h[:, 0, :], op=MULT)
            elif c_in == 0:
                nc.vector.tensor_tensor(out=out, in0=sums[s, c_in][:], in1=h[:, 1, :], op=MULT)
            else:
                nc.vector.scalar_tensor_tensor(
                    out=out, in0=sums[s, c_in][:], scalar=-1.0, in1=h[:, 1, :], op0=MULT, op1=MULT
                )

        def store_y(s):
            r, fg = divmod(s, F_GROUPS)
            nc.sync.dma_start(out=y_rows[r * P:(r + 1) * P, :, fg * KG:(fg + 1) * KG], in_=y[s][:])

        def add_terms(s):
            y[s] = work.tile([P, C, KG], F32, name="y", tag="y", bufs=4)
            nc.gpsimd.tensor_tensor(out=y[s][:], in0=terms[s][:, 0, :, :], in1=terms[s][:, 1, :, :], op=ADD)
            store_y(s)

        def round_y(s):
            y_bf[s] = work.tile([P, C, KG], BF16, name="y_bf", tag="y_bf", bufs=3, align_bytes=64)
            for c in range(C):
                nc.scalar.copy(
                    out=y_bf[s][:, c, :].rearrange("r (u p e) -> r u p e", u=2, e=2),
                    in_=y[s][:, c, :].rearrange("r (p u e) -> r u p e", u=2, e=2),
                )

        def turn_y(s):
            bank = psum.tile([P, C, 2, P], F32, name="turned", tag="turned", bufs=4)
            for c in range(C):
                words = y_bf[s][:, c, :].bitcast(F32)
                for u in range(2):
                    nc.tensor.transpose(bank[:, c, u, :], words[:, u * P:(u + 1) * P], ident[:])
            turned["y", s] = bank

        def copy_y(s):
            r, fg = divmod(s, F_GROUPS)
            bank = turned["y", s]
            grouped = y_grouped[:, fg, r * M_UNIT * 4:(r + 1) * M_UNIT * 4]
            nc.scalar.copy(
                out=grouped.bitcast(F32).rearrange("p (r w) -> p r w", w=2 * C),
                in_=bank[:].rearrange("p c u r -> p r (c u)"),
            )

        def quantise_y(fg, r0, r1):
            m0, m1 = r0 * M_UNIT, r1 * M_UNIT
            nc.vector.quantize_mx(
                out=y_codes[:, fg, m0:m1].bitcast(FP8X4),
                scales=y_scales[:, fg, m0:m1],
                in_=y_grouped[:, fg, 4 * m0:4 * m1],
            )

        def store_codes(fg, r0, r1):
            m0, m1 = r0 * M_UNIT, r1 * M_UNIT
            nc.sync.dma_start(
                out=out_1[fg].rearrange("p m t -> p (m t)")[:, 4 * m0:4 * m1].bitcast(I32),
                in_=y_codes[:, fg, m0:m1].bitcast(I32),
            )

        def store_scales(r0, r1, queues):
            m0, m1 = r0 * M_UNIT, r1 * M_UNIT
            for q in range(4):
                queues[q % len(queues)].dma_start(
                    out=out_2[:, 4 * q:4 * q + 4, m0:m1].rearrange("g r m -> r g m").bitcast(I32),
                    in_=y_scales[32 * q:32 * q + 4, :, m0:m1].bitcast(I32),
                )

        x_turns = {1: [2], 2: [3, 4], 4: [5], 5: [6], 8: [7]}
        x_quants = {2: (2, 3), 4: (3, 5), 8: (5, 7), 12: (7, 8)}
        y_quants = {}
        for r0 in range(0, ROW_TILES - 2, 2):
            y_quants[2 * r0 + 3] = (0, r0, r0 + 1)
            y_quants[2 * r0 + 5] = (0, r0 + 1, r0 + 2)
            y_quants[2 * r0 + 6] = (1, r0, r0 + 2)

        for g in range(K_GROUPS):
            turn_x(0, g, g + 1)
            copy_x(0, g, g + 1)
        for g in range(K_GROUPS):
            quantise_x(g, g + 1)
        turn_x(1, 0, K_GROUPS)
        copy_x(1, 0, K_GROUPS)
        quantise_x(K_GROUPS, 2 * K_GROUPS)
        multiply(0, 0)
        multiply(0, 1)

        for s in range(UNITS):
            if s >= 2:
                round_y(s - 2)
            if s >= 3:
                copy_y(s - 3)
            for r in x_turns.get(s - 1, []):
                copy_x(r, 0, K_GROUPS)
            if s + 1 < UNITS:
                multiply(s + 1, 0)
                multiply(s + 1, 1)
            for r in x_turns.get(s, []):
                turn_x(r, 0, K_GROUPS)
            if s >= 2:
                turn_y(s - 2)
            if s >= 1:
                add_terms(s - 1)
            for c_in in range(C):
                for c_out in range(C):
                    product(s, c_in, c_out)
            if s in x_quants:
                r0, r1 = x_quants[s]
                quantise_x(r0 * K_GROUPS, r1 * K_GROUPS)
            if s in y_quants:
                quantise_y(*y_quants[s])
                store_codes(*y_quants[s])
            if s == UNITS - 2:
                store_scales(0, ROW_TILES - 2, [nc.sync])

        last = UNITS - 1
        r_last = ROW_TILES - 1
        copy_y(last - 2)
        round_y(last - 1)
        y_bf[last] = work.tile([P, C, KG], BF16, name="y_bf", tag="y_bf", bufs=3, align_bytes=64)
        for c in range(C):
            nc.vector.tensor_tensor(
                out=y_bf[last][:, c, :].rearrange("r (u p e) -> r u p e", u=2, e=2),
                in0=terms[last][:, 0, c, :].rearrange("r (p u e) -> r u p e", u=2, e=2),
                in1=terms[last][:, 1, c, :].rearrange("r (p u e) -> r u p e", u=2, e=2),
                op=ADD,
            )
        y[last] = work.tile([P, C, KG], F32, name="y", tag="y", bufs=4)
        nc.vector.tensor_tensor(out=y[last][:], in0=terms[last][:, 0, :, :], in1=terms[last][:, 1, :, :], op=ADD)
        store_y(last)
        turn_y(last)
        copy_y(last)
        turn_y(last - 1)
        copy_y(last - 1)
        for fg in range(F_GROUPS):
            quantise_y(fg, r_last - 1, r_last)
        m0, m1 = (r_last - 1) * M_UNIT, r_last * M_UNIT
        nc.sync.dma_start(
            out=out_1.rearrange("g p m t -> p g (m t)")[:, :, 4 * m0:4 * m1].bitcast(I32),
            in_=y_codes[:, :, m0:m1].bitcast(I32),
        )
        for fg in (1, 0):
            quantise_y(fg, r_last, r_last + 1)
            store_codes(fg, r_last, r_last + 1)
        store_scales(ROW_TILES - 2, ROW_TILES, [nc.scalar, nc.sync])
